import numpy as np, ml_dtypes
CORES = [50,106,114,52,108,116]
N = 6
F = 64
def setup_inputs(rng):
    return {"ah": rng.standard_normal((N, 128, 128), dtype=np.float32).astype(ml_dtypes.bfloat16), "al": (rng.standard_normal((N, 128, 128), dtype=np.float32) / 256).astype(ml_dtypes.bfloat16), "bh": rng.standard_normal((N, 128, F), dtype=np.float32).astype(ml_dtypes.bfloat16), "bl": (rng.standard_normal((N, 128, F), dtype=np.float32) / 256).astype(ml_dtypes.bfloat16)}
def setup_inputs_big(rng):
    d = setup_inputs(rng)
    for k in ("ah", "al", "bh", "bl"): d[k] = (d[k].astype(np.float32) * 1024.0).astype(d[k].dtype)
    return d
def setup_inputs_small(rng):
    d = setup_inputs(rng)
    for k in ("ah", "al", "bh", "bl"): d[k] = (d[k].astype(np.float32) * (1 / 1024.0)).astype(d[k].dtype)
    return d
def setup_inputs_apart(rng):
    d = setup_inputs(rng)
    f = (10.0 ** rng.permutation(np.linspace(-1.5, 1.5, N))).astype(np.float32).reshape(N, 1, 1)
    for k in ("ah", "al", "bh", "bl"): d[k] = (d[k].astype(np.float32) * f).astype(d[k].dtype)
    return d
def reference(ah, al, bh, bl):
    AH, AL, BH, BL = ah.astype(np.float64), al.astype(np.float64), bh.astype(np.float64), bl.astype(np.float64)
    s = sum((AH[j] + AL[j]).T @ (BH[j] + BL[j]) for j in range(N))
    s = s.astype(np.float32 if ah.dtype != np.float64 else np.float64)
    return {"y": np.broadcast_to(s, (N,) + s.shape)}

from concourse.bass import DstId, RemoteDMATransfer
from concourse.mybir import AluOpType

PACK = 2
KP = 128 // PACK
M = 128
F = 64
K1 = 8
HELP = False

SCRATCH = {
    "sah": ("sbuf", [128, M * PACK], "bfloat16"),
    "sal": ("sbuf", [128, M * PACK], "bfloat16"),
    "sbh": ("sbuf", [128, F * PACK], "bfloat16"),
    "sbl": ("sbuf", [128, F * PACK], "bfloat16"),
    "ps0": ("psum", [128, 512], "float32"),
    "ps1": ("psum", [128, 512], "float32"),
    "ps2": ("psum", [128, 512], "float32"),
    "part": ("sbuf", [128, F], "float32"),
    "peer0": ("sbuf", [128, F], "float32"),
    "peer1": ("sbuf", [128, F], "float32"),
    "land0": ("sbuf", [128, F], "float32"),
    "land1": ("sbuf", [128, F], "float32"),
    "land2": ("sbuf", [128, F], "float32"),
    "res": ("sbuf", [128, F], "float32"),
}
SEMAPHORES = ["ldh", "lda", "ldb", "mm", "cp", "s1", "in0", "in1", "in2", "v1", "v2", "v3", "st", "snt"]


def _lowest(mask, k):
    out, n, b = 0, 0, 1
    while n < k:
        if mask & b:
            out |= b
            n += 1
        b <<= 1
    return out


def _count(mask):
    return bin(mask).count("1")


def _plan(T, topo):
    chips = []
    for c in T.cores:
        if topo.chip(c) not in chips:
            chips.append(topo.chip(c))
    members = {ch: [c for c in T.cores if topo.chip(c) == ch] for ch in chips}
    helpers = {ch: [] for ch in chips}
    sends = {c: [] for c in T.cores}

    def cands(pair):
        s, d = pair
        return [c for c in members[s] if all(topo.may_write(c, x) for x in members[d])]

    pairs = sorted([(s, d) for s in chips for d in chips if s != d], key=lambda p: len(cands(p)))
    for p in pairs:
        c = min(cands(p), key=lambda c: len(sends[c]))
        sends[c].append(p[1])
    if HELP:
        every = range(topo.CHIPS * topo.CORES_PER_CHIP)
        for c in list(sends):
            while len(sends[c]) > 1:
                d = sends[c][-1]
                idle = [h for h in every
                        if topo.chip(h) == topo.chip(c) and h not in T.cores and h not in sends
                        and all(topo.may_write(h, x) for x in members[d])]
                idle.sort(key=lambda h: topo.die(h) == topo.die(c))
                if not idle:
                    break
                sends[c].pop()
                sends[idle[0]] = [d]
                helpers[topo.chip(c)].append(idle[0])
    return chips, members, helpers, sends


def rank_program(g, core, T, topo):
    chips, members, helpers, sends = _plan(T, topo)
    rank = T.rank_of(core)
    if rank is None and core not in sends:
        return
    sem = T.sem
    mine = topo.chip(core)
    ci = chips.index(mine)

    def targets(c):
        return [x for d in sends.get(c, []) for x in members[d]]

    def near(c):
        return [x for x in members[topo.chip(c)] if x != c] + helpers[topo.chip(c)]

    def mask2(c):
        m = -1
        for x in targets(c):
            m &= topo.mask(c, x)
        return m

    def mask1(c):
        m = -1
        for x in near(c):
            m &= topo.mask(c, x)
        return (m & mask2(c)) if targets(c) else _lowest(m, K1)

    def slot(src, x):
        return [m for m in members[topo.chip(x)] if m != x].index(src)

    def ids(cs):
        return [DstId(rid=topo.addr(x)[0], pnc=topo.addr(x)[1]) for x in cs]

    got1 = sum(_count(mask1(m)) for m in members[mine] if m != core)
    sent = 0

    if rank is not None:
        g.sync.dma_start(T.sah[0:KP, :], T.ah[:]).then_inc(sem.ldh, 16)
        g.scalar.dma_start(T.sbh[0:KP, :], T.bh[:]).then_inc(sem.ldh, 16)
        g.scalar.dma_start(T.sbl[0:KP, :], T.bl[:]).then_inc(sem.ldb, 16)
        g.sync.dma_start(T.sal[0:KP, :], T.al[:]).then_inc(sem.lda, 16)

        terms = [(T.sah, T.sbh), (T.sah, T.sbl), (T.sal, T.sbh), (T.sal, T.sbl)]
        waits = [(sem.ldh, 32), (sem.ldb, 16), (sem.lda, 16), None]
        last = None
        for t, (a, b) in enumerate(terms):
            if waits[t] is not None:
                g.tensor.wait_ge(waits[t][0], waits[t][1])
            for q in range(PACK):
                last = g.tensor.matmul(T.ps0[:, 0:F], a[0:KP, q * M:(q + 1) * M], b[0:KP, q * F:(q + 1) * F],
                                       start=(t == 0 and q == 0), stop=(t == 3 and q == PACK - 1))
        last.then_inc(sem.mm, 1)
        g.vector.wait_ge(sem.mm, 1)
        g.vector.tensor_copy(T.part[:], T.ps0[:, 0:F]).then_inc(sem.cp, 1)

        g.wait_ge(sem.cp, 1)
        m1 = mask1(core)
        g.remote_dma_fused([RemoteDMATransfer(
            dst_ids=ids(near(core)), dma_engine_mask=m1, remote_sem=sem.s1,
            srcs=[T.part[:]], dsts=[T["peer%d" % slot(core, x)][:] for x in near(core)], alu_op=0)],
            local_sem=sem.snt)
        sent += _count(m1)
        srcs = [T.part[:], T.peer0[:]]
    else:
        srcs = [T.peer0[:], T.peer1[:]]

    if targets(core):
        g.wait_ge(sem.s1, got1)
        m2 = mask2(core)
        g.remote_dma_fused([RemoteDMATransfer(
            dst_ids=ids(targets(core)), dma_engine_mask=m2, remote_sem=sem["in%d" % ci],
            srcs=srcs, dsts=[T["land%d" % ci][:] for x in targets(core)], alu_op=1)],
            local_sem=sem.snt)
        sent += _count(m2)

    if rank is not None:
        g.vector.wait_ge(sem.s1, got1)
        g.vector.tensor_tensor(T.ps1[:, 0:F], T.ps0[:, 0:F], T.peer0[:], op=AluOpType.add).then_inc(sem.v1, 1)
        src_of = {topo.chip(c): c for c in sends if mine in sends[c]}
        order = sorted(src_of, key=lambda ch: (len(targets(src_of[ch])), not topo.same_plane(ch, mine)))
        steps = [(T.ps2[:, 0:F], T.ps1[:, 0:F], sem.v1, sem.v2), (T.res[:], T.ps2[:, 0:F], sem.v2, sem.v3)]
        for ch, (out, acc, before, after) in zip(order, steps):
            k = chips.index(ch)
            g.vector.wait_ge(sem["in%d" % k], _count(mask2(src_of[ch])))
            g.vector.wait_ge(before, 1)
            g.vector.tensor_tensor(out, acc, T["land%d" % k][:], op=AluOpType.add).then_inc(after, 1)
        g.sync.wait_ge(sem.v3, 1)
        g.sync.dma_start(T.y[:], T.res[:]).then_inc(sem.st, 16)
        g.sync.wait_ge(sem.st, 16)
    g.wait_ge(sem.snt, sent)
